import numpy as np
import ml_dtypes


def mxq(x, axis, fmt="e4m3"):
    dtype, down = {"e4m3": (ml_dtypes.float8_e4m3fn, 7), "e5m2": (ml_dtypes.float8_e5m2, 14)}[fmt]
    v = np.moveaxis(np.asarray(x, np.float32).astype(ml_dtypes.bfloat16).astype(np.float64), axis, -1)
    blocks = v.reshape(v.shape[:-1] + (-1, 32))
    amax = np.abs(blocks).max(-1, keepdims=True)
    byte = np.maximum(np.where(amax > 0, np.frexp(amax)[1] - 1 + 127, 0) - down, 1)
    scale = np.exp2(byte - 127.0)
    codes = (blocks / scale).astype(np.float32).astype(dtype).astype(np.float64)
    return np.moveaxis((codes * scale).reshape(v.shape), -1, axis)


WIDE = False


def mx_kscale(k):
    if not WIDE:
        return np.ones(k)
    levels = np.array([30, -30])
    if k % 512:
        return np.exp2(np.random.permutation(np.resize(levels, k // 32))).repeat(32)
    a = np.empty((k // 512, 16))
    for p in range(k // 512):
        a[p, :8] = np.random.permutation(np.resize(levels, 8))
        for g in range(8):
            far = levels[np.abs(levels - a[p, g]) >= 10]
            a[p, g + 8] = far[np.random.randint(len(far))]
    return np.exp2(a.ravel()).repeat(32)


BF16 = ml_dtypes.bfloat16


def bf(x):
    return np.asarray(x, np.float32).astype(BF16)


def f64(x):
    return np.asarray(x).astype(np.float64)


E2M1 = np.array([0.0, 0.5, 1.0, 1.5, 2.0, 3.0, 4.0, 6.0, -0.0, -0.5, -1.0, -1.5, -2.0, -3.0, -4.0, -6.0])


def pack_weight(w, fmt):
    k, n = w.shape
    w = f64(bf(w)).reshape(k // 32, 32, n)
    amax = np.abs(w).max(1)
    if fmt == "e4m3":
        byte = np.frexp(amax)[1] - 1 + 127 - 7
    else:
        mant, ex = np.frexp(amax / 6.0)
        byte = np.where(mant > 0.5, ex, ex - 1) + 127
    byte = np.clip(np.where(amax > 0, byte, 1), 1, 254)
    scaled = (w * np.exp2(127.0 - byte)[:, None, :]).reshape(k, n).astype(np.float32)
    by_word = np.ascontiguousarray(scaled.reshape(k // 512, 128, 4, n).transpose(0, 1, 3, 2))
    if fmt == "e4m3":
        words = by_word.astype(ml_dtypes.float8_e4m3fn).view(np.uint8)
    else:
        c = by_word.astype(ml_dtypes.float4_e2m1fn).view(np.uint8) & 0xF
        words = c[..., 0::2] | (c[..., 1::2] << 4)
    return np.ascontiguousarray(words), np.ascontiguousarray(byte.astype(np.uint8).reshape(k // 512, 16, n))


def unpack_weight(words, scales, fmt):
    g, p, n, _ = words.shape
    if fmt == "e4m3":
        vals = np.ascontiguousarray(words).view(ml_dtypes.float8_e4m3fn).astype(np.float64)
    else:
        nib = np.empty((g, p, n, 4), np.uint8)
        nib[..., 0::2] = words & 0xF
        nib[..., 1::2] = words >> 4
        vals = E2M1[nib]
    vals = vals * np.repeat(np.exp2(scales.astype(np.float64) - 127.0), 8, axis=1)[..., None]
    return vals.transpose(0, 1, 3, 2).reshape(g * 512, n)
def pack4(w):
    words, scales = pack_weight(w, "e2m1")
    return words.reshape(words.shape[0], 128, -1), scales


def unpack4(words, scales):
    return unpack_weight(words.reshape(words.shape[0], 128, -1, 2), scales, "e2m1")


M, NX, NU, F = 1024, 512, 1024, 1536


def setup_inputs():
    s = mx_kscale(NX)
    v = mx_kscale(NU)
    t = mx_kscale(F)
    x0 = np.random.standard_normal((M, NX)) * s
    u = np.random.standard_normal((M, NU)) * v
    phi = np.random.standard_normal((NX, F)) / np.sqrt(NX) / s[:, None]
    gamma = np.random.standard_normal((NU, F)) / np.sqrt(NU) / v[:, None]
    phi_words, phi_scales = pack4(phi)
    gamma_words, gamma_scales = pack4(gamma)
    return {"x0": bf(x0),
            "u": bf(u),
            "phi_words": phi_words, "phi_scales": phi_scales,
            "gamma_words": gamma_words, "gamma_scales": gamma_scales,
            "yref": bf(np.random.standard_normal((M, F))),
            "ywt": bf((1 + 0.1 * np.random.standard_normal(F)) * t),
            "adj": bf(np.random.standard_normal((F, NU)) / np.sqrt(F) / t[:, None]),
            "uwt": bf(0.5 * (1 + 0.1 * np.random.standard_normal(NU)) / v)}


def reference(x0, u, phi_words, phi_scales, gamma_words, gamma_scales, yref, ywt, adj, uwt):
    free = mxq(f64(x0), 1, "e4m3") @ unpack4(phi_words, phi_scales)
    forced = mxq(f64(u), 1, "e4m3") @ unpack4(gamma_words, gamma_scales)
    e = (free + forced - f64(yref)) * f64(ywt)
    back = mxq(e, 1, "e5m2") @ mxq(f64(adj), 0, "e4m3")
    return back + f64(uwt) * f64(u)

@@ -1,0 +1,299 @@
+from contextlib import ExitStack
+
+import concourse.mybir as mybir
+from concourse.masks import make_identity
+
+M, NX, NU, F = 1024, 512, 1024, 1536
+FLOPS = 2 * M * (NX + NU) * F + 2 * M * F * NU
+
+F32 = mybir.dt.float32
+BF16 = mybir.dt.bfloat16
+I32 = mybir.dt.int32
+U32 = mybir.dt.uint32
+U8 = mybir.dt.uint8
+E4M3 = mybir.dt.float8_e4m3fn_x4
+E5M2 = mybir.dt.float8_e5m2_x4
+E2M1 = mybir.dt.float4_e2m1fn_x4
+ALU = mybir.AluOpType
+
+P = 128
+KP = 512
+N = 512
+TILES = M // P
+PASSES = 3
+CHUNKS = F // N
+HALVES = NU // N
+
+
+def tile_condensed_mpc_update_direction_s9_kernel(
+    tc, x0, u, phi_words, phi_scales, gamma_words, gamma_scales, yref, ywt, adj, uwt, out
+):
+    nc = tc.nc
+    with ExitStack() as ctx:
+        keep = ctx.enter_context(tc.tile_pool(name="keep", bufs=1))
+        work = ctx.enter_context(tc.tile_pool(name="work", bufs=4))
+        psum = ctx.enter_context(tc.psum_pool(name="psum", bufs=8))
+        ctx.enter_context(tc.manual_schedule())
+
+        def kept(name, shape, dtype):
+            return keep.tile(shape, dtype, name=name, align_bytes=64)
+
+        def staged(name, shape, dtype):
+            return work.tile(shape, dtype, name=name, align_bytes=64)
+
+        def new_bank():
+            return psum.tile([P, N], F32, name="bank")
+
+        ident = kept("ident", [P, P], F32)
+
+        phi_plane = kept("phi_plane", [P, F], U8)
+        gamma_plane = kept("gamma_plane", [P, 2, F], U8)
+        nc.vector.memset(gamma_plane[:].bitcast(I32), 0)
+        nc.vector.memset(phi_plane[:].bitcast(I32), 0)
+        make_identity(nc, ident[:])
+
+        x_sb = [kept("x%d" % j, [P, NX], BF16) for j in range(TILES)]
+        u_sb = [kept("u%d" % j, [P, NU], BF16) for j in range(TILES)]
+        y_sb = [kept("y%d" % j, [P, F], BF16) for j in range(TILES)]
+        phi_sb = kept("phi", [P, 2 * F], U8)
+        gamma_sb = kept("gamma", [P, 2, 2 * F], U8)
+        adj_sb = [kept("adj%d" % c, [P, 4, N], BF16) for c in range(HALVES * PASSES)]
+        adj_codes = [kept("adjc%d" % c, [P, N], U32) for c in range(HALVES * PASSES)]
+        adj_scales = [kept("adjs%d" % c, [P, N], U8) for c in range(HALVES * PASSES)]
+        ywt_cols = kept("ywt_cols", [P, PASSES * 4], BF16)
+        uwt_cols = kept("uwt_cols", [P, 8], BF16)
+        ywt_rows = kept("ywt_rows", [P, F], BF16)
+        uwt_rows = kept("uwt_rows", [P, NU], BF16)
+        wide = [kept("wide%d" % j, [P, F], F32) for j in range(TILES)]
+        e_codes = [kept("ec%d" % j, [P, PASSES * P], U32) for j in range(TILES)]
+        e_scales = [kept("es%d" % j, [P, PASSES * P], U8) for j in range(TILES)]
+        x_codes, x_scales, x_grouped, e_grouped, e_sb, adj_grouped, penalties = {}, {}, {}, {}, {}, {}, {}
+
+        def rows(j):
+            return slice(j * P, (j + 1) * P)
+
+        def load_xu(j):
+            nc.sync.dma_start(out=x_sb[j][:], in_=x0[rows(j), :])
+            nc.sync.dma_start(out=u_sb[j][:], in_=u[rows(j), :])
+
+        def load_y(j):
+            nc.sync.dma_start(out=y_sb[j][:], in_=yref[rows(j), :])
+
+        def load_adj(c):
+            h, g = divmod(c, PASSES)
+            src = adj[g * KP : (g + 1) * KP, h * N : (h + 1) * N].rearrange("(p t) n -> p t n", t=4)
+            nc.sync.dma_start(out=adj_sb[c][:], in_=src)
+
+        load_xu(0)
+        nc.sync.dma_start(
+            out=ywt_cols[:].rearrange("q (g e) -> q g e", e=4), in_=ywt.rearrange("(g q e) -> q g e", q=P, e=4)
+        )
+        for r in range(4):
+            src = gamma_scales.rearrange("g q n -> q g n")[r:16:4, :, :]
+            nc.sync.dma_start(out=gamma_plane[r:P:32, :, :].bitcast(I32), in_=src.bitcast(I32))
+        nc.sync.dma_start(out=gamma_sb[:].bitcast(I32), in_=gamma_words.rearrange("g p b -> p g b").bitcast(I32))
+        nc.sync.dma_start(out=phi_sb[:].bitcast(I32), in_=phi_words[0].bitcast(I32))
+        for r in range(4):
+            nc.sync.dma_start(out=phi_plane[r:P:32, :].bitcast(I32), in_=phi_scales[0][r:16:4, :].bitcast(I32))
+        nc.gpsimd.dma_start(out=uwt_cols[:], in_=uwt.rearrange("(n e) -> n e", e=8))
+        load_y(0)
+        load_xu(1)
+        load_xu(2)
+        for j in range(1, 4):
+            load_y(j)
+            load_adj(2 * j - 2)
+            load_xu(j + 2)
+            load_adj(2 * j - 1)
+        for j in range(4, TILES):
+            load_y(j)
+            if j + 2 < TILES:
+                load_xu(j + 2)
+
+        def x_pairs(j):
+            x_grouped[j] = staged("x_grouped", [P, PASSES * KP], BF16)
+            xw = x_sb[j][:].bitcast(F32)
+            uw = u_sb[j][:].bitcast(F32)
+            srcs = [[xw[:, w:256:2] for w in range(2)]]
+            srcs += [[uw[:, 256 * g + w : 256 * (g + 1) : 2] for w in range(2)] for g in range(2)]
+            return [(srcs[g], x_grouped[j], g, True) for g in range(PASSES)]
+
+        def e_pairs(j):
+            e_grouped[j] = staged("e_grouped", [P, PASSES * KP], BF16)
+            ew = e_sb[j][:].bitcast(F32)
+            return [([ew[:, 256 * g + P * w : 256 * g + P * (w + 1)] for w in range(2)], e_grouped[j], g, True) for g in range(PASSES)]
+
+        def ywt_pairs():
+            cols = ywt_cols[:].bitcast(F32)
+            return [([cols[:, 2 * g + w : 2 * g + w + 1].to_broadcast([P, P]) for w in range(2)], ywt_rows, g, False) for g in range(PASSES)]
+
+        def transpose_run(pairs):
+            copies = []
+            for b in range(0, len(pairs), 2):
+                bank = new_bank()
+                group = pairs[b : b + 2]
+                for s, pair in enumerate(group):
+                    for w in range(2):
+                        nc.tensor.transpose(bank[:, 256 * s + P * w : 256 * s + P * (w + 1)], pair[0][w], ident[:])
+                if len(group) == 2 and group[0][1] is group[1][1]:
+                    copies.append((bank, 0, 2, group[0]))
+                else:
+                    copies.extend((bank, s, 1, pair) for s, pair in enumerate(group))
+            return copies
+
+        def copy_out(copies):
+            for bank, s, count, (srcs, dst, g, interleave) in copies:
+                src = bank[:, 256 * s : 256 * (s + count)]
+                words = dst[:].bitcast(F32)[:, 256 * g : 256 * (g + count)]
+                if interleave:
+                    nc.scalar.copy(
+                        out=words.rearrange("p (g r w) -> p g r w", w=2, r=P), in_=src.rearrange("p (g w r) -> p g r w", w=2, r=P)
+                    )
+                else:
+                    nc.scalar.copy(out=words, in_=src)
+
+        def spread_uwt():
+            bank = new_bank()
+            cols = uwt_cols[:].bitcast(F32)
+            for c in range(4):
+                nc.tensor.transpose(bank[:, P * c : P * (c + 1)], cols[:, c : c + 1].to_broadcast([P, P]), ident[:])
+            return bank
+
+        def copy_uwt(bank):
+            nc.scalar.copy(
+                out=uwt_rows[:].bitcast(F32).rearrange("p (n c) -> p n c", c=4), in_=bank[:].rearrange("p (c n) -> p n c", c=4)
+            )
+
+        def quantize(codes, scales, grouped, fmt, spans):
+            for a, b in spans:
+                nc.vector.quantize_mx(
+                    out=codes[:, P * a : P * b].bitcast(fmt), scales=scales[:, P * a : P * b], in_=grouped[:, KP * a : KP * b]
+                )
+
+        def quantize_x(j):
+            x_codes[j] = staged("x_codes", [P, PASSES * P], U32)
+            x_scales[j] = staged("x_scales", [P, PASSES * P], U8)
+            quantize(x_codes[j], x_scales[j], x_grouped[j], E4M3, [(0, 2), (2, 3)])
+
+        def quantize_e(j):
+            quantize(e_codes[j], e_scales[j], e_grouped[j], E5M2, [(0, 1), (1, 3)])
+
+        def interleave_adj(c):
+            adj_grouped[c] = staged("adj_grouped", [P, 4 * N], BF16)
+            nc.scalar.copy(
+                out=adj_grouped[c][:].rearrange("p (c i t) -> p c t i", i=4, t=4),
+                in_=adj_sb[c][:].rearrange("p t (c i) -> p c t i", i=4),
+            )
+
+        def quantize_adj(c):
+            nc.vector.quantize_mx(out=adj_codes[c][:].bitcast(E4M3), scales=adj_scales[c][:], in_=adj_grouped[c][:])
+
+        def predict(j, chunks=range(CHUNKS), after=None):
+            for n in chunks:
+                bank = new_bank()
+                cols = slice(n * N, (n + 1) * N)
+                for g in (1, 2, 0):
+                    byte_cols = slice(2 * N * n, 2 * N * (n + 1))
+                    words = phi_sb[:, byte_cols] if g == 0 else gamma_sb[:, g - 1, byte_cols]
+                    plane = phi_plane[:, cols] if g == 0 else gamma_plane[:, g - 1, cols]
+                    nc.tensor.matmul_mx(
+                        out=bank[:],
+                        lhsT=x_codes[j][:, P * g : P * (g + 1)].bitcast(E4M3),
+                        lhsT_scale=x_scales[j][:, P * g : P * (g + 1)],
+                        rhs=words.bitcast(E2M1),
+                        rhs_scale=plane,
+                        start=(g == 1),
+                        stop=(g == 0),
+                    )
+                nc.vector.tensor_tensor(
+                    out=wide[j][:, cols].rearrange("p (w q b) -> p w q b", w=2, b=2),
+                    in0=bank[:].rearrange("p (q w b) -> p w q b", w=2, b=2),
+                    in1=y_sb[j][:, cols].rearrange("p (q w b) -> p w q b", w=2, b=2),
+                    op=ALU.subtract,
+                )
+
+        def weigh(j, first=0, last=CHUNKS):
+            if first == 0:
+                e_sb[j] = staged("e_sb", [P, F], BF16)
+            cols = slice(first * N, last * N)
+            nc.vector.tensor_tensor(out=e_sb[j][:, cols], in0=wide[j][:, cols], in1=ywt_rows[:, cols], op=ALU.mult)
+
+        def penalty(unit, home):
+            j, h = unit
+            cols = slice(h * N, (h + 1) * N)
+            penalties[unit] = home
+            nc.gpsimd.tensor_tensor(out=home, in0=u_sb[j][:, cols], in1=uwt_rows[:, cols], op=ALU.mult)
+
+        def back_project(j, h):
+            bank = new_bank()
+            for g in range(PASSES):
+                nc.tensor.matmul_mx(
+                    out=bank[:],
+                    lhsT=e_codes[j][:, P * g : P * (g + 1)].bitcast(E5M2),
+                    lhsT_scale=e_scales[j][:, P * g : P * (g + 1)],
+                    rhs=adj_codes[PASSES * h + g][:].bitcast(E4M3),
+                    rhs_scale=adj_scales[PASSES * h + g][:],
+                    start=(g == 0),
+                    stop=(g == PASSES - 1),
+                )
+            return bank
+
+        def finish(j, h, bank):
+            home = penalties[(j, h)]
+            nc.vector.tensor_tensor(out=home, in0=bank[:], in1=home, op=ALU.add)
+            nc.sync.dma_start(out=out[rows(j), h * N : (h + 1) * N], in_=home)
+
+        interleave_at = {1: [0, 1], 2: [2, 3], 3: [4, 5]}
+        quantize_at = {2: [0], 3: [1, 2], 4: [3, 4], 5: [5]}
+        units_at = {3: [(0, 0)], 4: [(1, 0)], 5: [(2, 0), (0, 1), (1, 1)], 6: [(2, 1), (3, 0), (3, 1)], 7: [(4, 0), (4, 1)]}
+        order = [x for i in sorted(units_at) for x in units_at[i]]
+        order = order + [(j, h) for j in range(TILES) for h in range(HALVES) if (j, h) not in order]
+        share = [1, 1, 2, 2, 3, 3, 2, 2]
+
+        def release(j):
+            first = sum(share[:j])
+            for s in range(share[j]):
+                slot = CHUNKS - 1 - s
+                penalty(order[first + s], wide[j][:, slot * N : (slot + 1) * N])
+
+        def project(units):
+            for j, h in units:
+                finish(j, h, back_project(j, h))
+
+        copy_out(transpose_run(x_pairs(0)))
+        quantize_x(0)
+        copy_out(transpose_run(ywt_pairs()))
+        predict(0, [0, 1])
+        copy_out(transpose_run(x_pairs(1)))
+        weigh(0, 0, 2)
+        predict(0, [2])
+        for i in range(1, TILES):
+            pairs = x_pairs(i + 1) if i + 1 < TILES else []
+            if i >= 2:
+                pairs = pairs + e_pairs(i - 2)
+            copies = transpose_run(pairs)
+            if i == 1:
+                copy_uwt(spread_uwt())
+            quantize_x(i)
+            if i >= 3:
+                quantize_e(i - 3)
+            for c in quantize_at.get(i, []):
+                quantize_adj(c)
+            weigh(i - 1, 2 if i == 1 else 0)
+            release(i - 1)
+            copy_out(copies)
+            for c in interleave_at.get(i, []):
+                interleave_adj(c)
+            predict(i)
+            project(units_at.get(i, []))
+        copy_out(transpose_run(e_pairs(6)))
+        quantize_e(5)
+        weigh(7)
+        banks = [back_project(5, h) for h in range(HALVES)]
+        copy_out(transpose_run(e_pairs(7)))
+        quantize_e(6)
+        release(7)
+        for h in range(HALVES):
+            finish(5, h, banks[h])
+        project([(6, 0)])
+        quantize_e(7)
+        project([(6, 1), (7, 0), (7, 1)])

@@ -31,8 +31,9 @@ def tile_condensed_mpc_update_direction_s9_kernel(
     nc = tc.nc
     with ExitStack() as ctx:
         keep = ctx.enter_context(tc.tile_pool(name="keep", bufs=1))
-        work = ctx.enter_context(tc.tile_pool(name="work", bufs=4))
-        psum = ctx.enter_context(tc.psum_pool(name="psum", bufs=8))
+        work = ctx.enter_context(tc.tile_pool(name="work", bufs=3))
+        psum = ctx.enter_context(tc.psum_pool(name="psum", bufs=6))
+        psum_kept = ctx.enter_context(tc.psum_pool(name="psum_kept", bufs=1))
         ctx.enter_context(tc.manual_schedule())
 
         def kept(name, shape, dtype):
@@ -48,9 +49,9 @@ def tile_condensed_mpc_update_direction_s9_kernel(
 
         phi_plane = kept("phi_plane", [P, F], U8)
         gamma_plane = kept("gamma_plane", [P, 2, F], U8)
-        nc.vector.memset(gamma_plane[:].bitcast(I32), 0)
         nc.vector.memset(phi_plane[:].bitcast(I32), 0)
         make_identity(nc, ident[:])
+        nc.vector.memset(gamma_plane[:].bitcast(I32), 0)
 
         x_sb = [kept("x%d" % j, [P, NX], BF16) for j in range(TILES)]
         u_sb = [kept("u%d" % j, [P, NU], BF16) for j in range(TILES)]
@@ -62,12 +63,13 @@ def tile_condensed_mpc_update_direction_s9_kernel(
         adj_scales = [kept("adjs%d" % c, [P, N], U8) for c in range(HALVES * PASSES)]
         ywt_cols = kept("ywt_cols", [P, PASSES * 4], BF16)
         uwt_cols = kept("uwt_cols", [P, 8], BF16)
-        ywt_rows = kept("ywt_rows", [P, F], BF16)
         uwt_rows = kept("uwt_rows", [P, NU], BF16)
-        wide = [kept("wide%d" % j, [P, F], F32) for j in range(TILES)]
         e_codes = [kept("ec%d" % j, [P, PASSES * P], U32) for j in range(TILES)]
         e_scales = [kept("es%d" % j, [P, PASSES * P], U8) for j in range(TILES)]
-        x_codes, x_scales, x_grouped, e_grouped, e_sb, adj_grouped, penalties = {}, {}, {}, {}, {}, {}, {}
+        x_codes, x_scales, x_sorted, e_sb, adj_grouped, penalties, wide = {}, {}, {}, {}, {}, {}, {}
+        x_grouped = [kept("xg%d" % j, [P, PASSES * KP], BF16) for j in range(TILES)]
+        e_grouped = [kept("eg%d" % j, [P, PASSES * KP], BF16) for j in range(TILES)]
+        ywt_banks = [psum_kept.tile([P, N], F32, name="ywt_bank%d" % b) for b in range(2)]
 
         def rows(j):
             return slice(j * P, (j + 1) * P)
@@ -79,52 +81,76 @@ def tile_condensed_mpc_update_direction_s9_kernel(
         def load_y(j):
             nc.sync.dma_start(out=y_sb[j][:], in_=yref[rows(j), :])
 
+        def load_phi():
+            for r in range(4):
+                nc.sync.dma_start(out=phi_plane[r:P:32, :].bitcast(I32), in_=phi_scales[0][r:16:4, :].bitcast(I32))
+            nc.sync.dma_start(out=phi_sb[:].bitcast(I32), in_=phi_words[0].bitcast(I32))
+
+        def load_gamma():
+            nc.sync.dma_start(out=gamma_sb[:].bitcast(I32), in_=gamma_words.rearrange("g p b -> p g b").bitcast(I32))
+            for r in range(4):
+                src = gamma_scales.rearrange("g q n -> q g n")[r:16:4, :, :]
+                nc.sync.dma_start(out=gamma_plane[r:P:32, :, :].bitcast(I32), in_=src.bitcast(I32))
+
+        def load_ywt():
+            src = ywt.rearrange("(g q e) -> q g e", q=P, e=4)
+            nc.sync.dma_start(out=ywt_cols[:].rearrange("q (g e) -> q g e", e=4), in_=src)
+
+        def load_uwt():
+            nc.sync.dma_start(out=uwt_cols[:], in_=uwt.rearrange("(n e) -> n e", e=8))
+
         def load_adj(c):
             h, g = divmod(c, PASSES)
             src = adj[g * KP : (g + 1) * KP, h * N : (h + 1) * N].rearrange("(p t) n -> p t n", t=4)
             nc.sync.dma_start(out=adj_sb[c][:], in_=src)
 
         load_xu(0)
-        nc.sync.dma_start(
-            out=ywt_cols[:].rearrange("q (g e) -> q g e", e=4), in_=ywt.rearrange("(g q e) -> q g e", q=P, e=4)
-        )
-        for r in range(4):
-            src = gamma_scales.rearrange("g q n -> q g n")[r:16:4, :, :]
-            nc.sync.dma_start(out=gamma_plane[r:P:32, :, :].bitcast(I32), in_=src.bitcast(I32))
-        nc.sync.dma_start(out=gamma_sb[:].bitcast(I32), in_=gamma_words.rearrange("g p b -> p g b").bitcast(I32))
-        nc.sync.dma_start(out=phi_sb[:].bitcast(I32), in_=phi_words[0].bitcast(I32))
-        for r in range(4):
-            nc.sync.dma_start(out=phi_plane[r:P:32, :].bitcast(I32), in_=phi_scales[0][r:16:4, :].bitcast(I32))
-        nc.gpsimd.dma_start(out=uwt_cols[:], in_=uwt.rearrange("(n e) -> n e", e=8))
-        load_y(0)
+        load_phi()
+        load_ywt()
+        load_gamma()
         load_xu(1)
+        load_y(0)
+        load_uwt()
+        load_adj(0)
         load_xu(2)
-        for j in range(1, 4):
+        load_y(1)
+        load_adj(1)
+        for j in range(2, 6):
+            load_xu(j + 1)
+            load_adj(j)
             load_y(j)
-            load_adj(2 * j - 2)
-            load_xu(j + 2)
-            load_adj(2 * j - 1)
-        for j in range(4, TILES):
-            load_y(j)
-            if j + 2 < TILES:
-                load_xu(j + 2)
+        load_xu(7)
+        load_y(6)
+        load_y(7)
 
         def x_pairs(j):
-            x_grouped[j] = staged("x_grouped", [P, PASSES * KP], BF16)
             xw = x_sb[j][:].bitcast(F32)
             uw = u_sb[j][:].bitcast(F32)
             srcs = [[xw[:, w:256:2] for w in range(2)]]
             srcs += [[uw[:, 256 * g + w : 256 * (g + 1) : 2] for w in range(2)] for g in range(2)]
+            if j in x_sorted:
+                srcs = [[x_sorted[j][:, 256 * g + P * w : 256 * g + P * (w + 1)] for w in range(2)] for g in range(PASSES)]
             return [(srcs[g], x_grouped[j], g, True) for g in range(PASSES)]
 
         def e_pairs(j):
-            e_grouped[j] = staged("e_grouped", [P, PASSES * KP], BF16)
             ew = e_sb[j][:].bitcast(F32)
             return [([ew[:, 256 * g + P * w : 256 * g + P * (w + 1)] for w in range(2)], e_grouped[j], g, True) for g in range(PASSES)]
 
-        def ywt_pairs():
+        def spread_ywt():
             cols = ywt_cols[:].bitcast(F32)
-            return [([cols[:, 2 * g + w : 2 * g + w + 1].to_broadcast([P, P]) for w in range(2)], ywt_rows, g, False) for g in range(PASSES)]
+            for c in range(2 * PASSES):
+                nc.tensor.transpose(ywt_banks[c // 4][:, P * (c % 4) : P * (c % 4 + 1)], cols[:, c : c + 1].to_broadcast([P, P]), ident[:])
+
+        def sort_words(j):
+            x_sorted[j] = staged("x_sorted", [P, PASSES * 256], F32)
+            nc.scalar.copy(
+                out=x_sorted[j][:, :256].rearrange("p (w q) -> p w q", w=2),
+                in_=x_sb[j][:].bitcast(F32).rearrange("p (q w) -> p w q", w=2),
+            )
+            nc.scalar.copy(
+                out=x_sorted[j][:, 256:].rearrange("p (g w q) -> p g w q", g=2, w=2),
+                in_=u_sb[j][:].bitcast(F32).rearrange("p (g q w) -> p g w q", g=2, w=2),
+            )
 
         def transpose_run(pairs):
             copies = []
@@ -169,59 +195,72 @@ def tile_condensed_mpc_update_direction_s9_kernel(
                     out=codes[:, P * a : P * b].bitcast(fmt), scales=scales[:, P * a : P * b], in_=grouped[:, KP * a : KP * b]
                 )
 
-        def quantize_x(j):
+        def quantize_x(j, spans=((0, 2), (2, 3))):
             x_codes[j] = staged("x_codes", [P, PASSES * P], U32)
             x_scales[j] = staged("x_scales", [P, PASSES * P], U8)
-            quantize(x_codes[j], x_scales[j], x_grouped[j], E4M3, [(0, 2), (2, 3)])
+            quantize(x_codes[j], x_scales[j], x_grouped[j], E4M3, spans)
 
         def quantize_e(j):
             quantize(e_codes[j], e_scales[j], e_grouped[j], E5M2, [(0, 1), (1, 3)])
 
-        def interleave_adj(c):
-            adj_grouped[c] = staged("adj_grouped", [P, 4 * N], BF16)
+        def interleave_adj(piece):
+            c, part = divmod(piece, 2)
+            if part == 0:
+                adj_grouped[c] = staged("adj_grouped", [P, 4 * N], BF16)
+            cols = slice(part * N // 2, (part + 1) * N // 2)
             nc.scalar.copy(
-                out=adj_grouped[c][:].rearrange("p (c i t) -> p c t i", i=4, t=4),
-                in_=adj_sb[c][:].rearrange("p t (c i) -> p c t i", i=4),
+                out=adj_grouped[c][:, 2 * N * part : 2 * N * (part + 1)].rearrange("p (c i t) -> p c t i", i=4, t=4),
+                in_=adj_sb[c][:, :, cols].rearrange("p t (c i) -> p c t i", i=4),
             )
 
         def quantize_adj(c):
             nc.vector.quantize_mx(out=adj_codes[c][:].bitcast(E4M3), scales=adj_scales[c][:], in_=adj_grouped[c][:])
 
-        def predict(j, chunks=range(CHUNKS), after=None):
+        def predict_pass(bank, j, n, g):
+            cols = slice(n * N, (n + 1) * N)
+            byte_cols = slice(2 * N * n, 2 * N * (n + 1))
+            words = phi_sb[:, byte_cols] if g == 0 else gamma_sb[:, g - 1, byte_cols]
+            plane = phi_plane[:, cols] if g == 0 else gamma_plane[:, g - 1, cols]
+            nc.tensor.matmul_mx(
+                out=bank[:],
+                lhsT=x_codes[j][:, P * g : P * (g + 1)].bitcast(E4M3),
+                lhsT_scale=x_scales[j][:, P * g : P * (g + 1)],
+                rhs=words.bitcast(E2M1),
+                rhs_scale=plane,
+                start=(g == 0),
+                stop=(g == PASSES - 1),
+            )
+
+        def subtract_reference(bank, j, n):
+            if n == 0:
+                wide[j] = staged("wide", [P, F], F32)
+            cols = slice(n * N, (n + 1) * N)
+            nc.vector.tensor_tensor(
+                out=wide[j][:, cols].rearrange("p (w q b) -> p w q b", w=2, b=2),
+                in0=bank[:].rearrange("p (q w b) -> p w q b", w=2, b=2),
+                in1=y_sb[j][:, cols].rearrange("p (q w b) -> p w q b", w=2, b=2),
+                op=ALU.subtract,
+            )
+
+        def predict(j, chunks=range(CHUNKS)):
             for n in chunks:
                 bank = new_bank()
-                cols = slice(n * N, (n + 1) * N)
-                for g in (1, 2, 0):
-                    byte_cols = slice(2 * N * n, 2 * N * (n + 1))
-                    words = phi_sb[:, byte_cols] if g == 0 else gamma_sb[:, g - 1, byte_cols]
-                    plane = phi_plane[:, cols] if g == 0 else gamma_plane[:, g - 1, cols]
-                    nc.tensor.matmul_mx(
-                        out=bank[:],
-                        lhsT=x_codes[j][:, P * g : P * (g + 1)].bitcast(E4M3),
-                        lhsT_scale=x_scales[j][:, P * g : P * (g + 1)],
-                        rhs=words.bitcast(E2M1),
-                        rhs_scale=plane,
-                        start=(g == 1),
-                        stop=(g == 0),
-                    )
-                nc.vector.tensor_tensor(
-                    out=wide[j][:, cols].rearrange("p (w q b) -> p w q b", w=2, b=2),
-                    in0=bank[:].rearrange("p (q w b) -> p w q b", w=2, b=2),
-                    in1=y_sb[j][:, cols].rearrange("p (q w b) -> p w q b", w=2, b=2),
-                    op=ALU.subtract,
-                )
+                for g in range(PASSES):
+                    predict_pass(bank, j, n, g)
+                subtract_reference(bank, j, n)
 
-        def weigh(j, first=0, last=CHUNKS):
-            if first == 0:
+        def weigh(j, b):
+            if b == 0:
                 e_sb[j] = staged("e_sb", [P, F], BF16)
-            cols = slice(first * N, last * N)
-            nc.vector.tensor_tensor(out=e_sb[j][:, cols], in0=wide[j][:, cols], in1=ywt_rows[:, cols], op=ALU.mult)
+            cols = slice(2 * N * b, min(2 * N * (b + 1), F))
+            weights = ywt_banks[b][:].bitcast(BF16)[:, : cols.stop - cols.start]
+            nc.vector.tensor_tensor(out=e_sb[j][:, cols], in0=wide[j][:, cols], in1=weights, op=ALU.mult)
 
-        def penalty(unit, home):
+        def penalty(engine, unit, home):
             j, h = unit
             cols = slice(h * N, (h + 1) * N)
             penalties[unit] = home
-            nc.gpsimd.tensor_tensor(out=home, in0=u_sb[j][:, cols], in1=uwt_rows[:, cols], op=ALU.mult)
+            engine.tensor_tensor(out=home, in0=u_sb[j][:, cols], in1=uwt_rows[:, cols], op=ALU.mult)
 
         def back_project(j, h):
             bank = new_bank()
@@ -242,58 +281,90 @@ def tile_condensed_mpc_update_direction_s9_kernel(
             nc.vector.tensor_tensor(out=home, in0=bank[:], in1=home, op=ALU.add)
             nc.sync.dma_start(out=out[rows(j), h * N : (h + 1) * N], in_=home)
 
-        interleave_at = {1: [0, 1], 2: [2, 3], 3: [4, 5]}
-        quantize_at = {2: [0], 3: [1, 2], 4: [3, 4], 5: [5]}
-        units_at = {3: [(0, 0)], 4: [(1, 0)], 5: [(2, 0), (0, 1), (1, 1)], 6: [(2, 1), (3, 0), (3, 1)], 7: [(4, 0), (4, 1)]}
+        interleave_at = {-1: [0, 1], 0: [2, 3, 4], 1: [5, 6, 7], 2: [8, 9, 10], 3: [11]}
+        quantize_at = {0: [0], 1: [1], 2: [2], 3: [3, 4], 4: [5]}
+        units_at = {3: [(0, 0)], 4: [(1, 0)], 5: [(2, 0), (0, 1), (1, 1)], 6: [(3, 0), (2, 1), (3, 1)], 7: [(4, 0), (4, 1), (5, 0), (5, 1)]}
         order = [x for i in sorted(units_at) for x in units_at[i]]
         order = order + [(j, h) for j in range(TILES) for h in range(HALVES) if (j, h) not in order]
-        share = [1, 1, 2, 2, 3, 3, 2, 2]
+        share = [1, 2, 3, 2, 3, 3, 2, 0]
+        sort_from = 9
 
-        def release(j):
-            first = sum(share[:j])
-            for s in range(share[j]):
-                slot = CHUNKS - 1 - s
-                penalty(order[first + s], wide[j][:, slot * N : (slot + 1) * N])
+        def release(i, homes):
+            first = sum(share[:i])
+            for s in range(share[i]):
+                penalty(nc.gpsimd, order[first + s], homes[s])
+
+        def as_home(grouped):
+            return grouped[:].bitcast(F32)[:, N // 2 :]
 
         def project(units):
             for j, h in units:
                 finish(j, h, back_project(j, h))
 
-        copy_out(transpose_run(x_pairs(0)))
-        quantize_x(0)
-        copy_out(transpose_run(ywt_pairs()))
-        predict(0, [0, 1])
-        copy_out(transpose_run(x_pairs(1)))
-        weigh(0, 0, 2)
-        predict(0, [2])
-        for i in range(1, TILES):
-            pairs = x_pairs(i + 1) if i + 1 < TILES else []
-            if i >= 2:
-                pairs = pairs + e_pairs(i - 2)
-            copies = transpose_run(pairs)
-            if i == 1:
-                copy_uwt(spread_uwt())
-            quantize_x(i)
-            if i >= 3:
-                quantize_e(i - 3)
+        first_pairs = x_pairs(0)
+        copy_out(transpose_run(first_pairs[:1]) + transpose_run(first_pairs[1:]))
+        quantize_x(0, ((0, 1), (1, 3)))
+        banks = [new_bank() for n in range(CHUNKS)]
+        for n in range(CHUNKS):
+            predict_pass(banks[n], 0, n, 0)
+        for n in range(CHUNKS):
+            for g in range(1, PASSES):
+                predict_pass(banks[n], 0, n, g)
+            subtract_reference(banks[n], 0, n)
+            if n == 0:
+                copy_out(transpose_run(x_pairs(1)))
+            if n == 1:
+                quantize_x(1)
+        spread_ywt()
+        for c in interleave_at[-1]:
+            interleave_adj(c)
+        copy_uwt(spread_uwt())
+        weigh(0, 0)
+        weigh(0, 1)
+        predict(1, [0])
+        copy_out(transpose_run(x_pairs(2)))
+        for c in interleave_at.get(0, []):
+            interleave_adj(c)
+        predict(1, [1])
+        for c in quantize_at.get(0, []):
+            quantize_adj(c)
+        quantize_x(2)
+        release(0, [as_home(x_grouped[2]), as_home(x_grouped[1])])
+        predict(1, [2])
+        for i in range(1, TILES - 1):
+            if i > 1:
+                predict(i)
+            weigh(i, 0)
+            weigh(i, 1)
+            project(units_at.get(i, []))
+            pairs = x_pairs(i + 2) + e_pairs(i - 1) if i + 2 < TILES else e_pairs(i - 1) + e_pairs(i)
+            copy_out(transpose_run(pairs))
+            homes = []
             for c in quantize_at.get(i, []):
                 quantize_adj(c)
-            weigh(i - 1, 2 if i == 1 else 0)
-            release(i - 1)
-            copy_out(copies)
+            if i >= 2:
+                quantize_e(i - 2)
+                homes = [as_home(e_grouped[i - 2])] + homes
+            if i + 2 < TILES:
+                quantize_x(i + 2)
+                homes = [as_home(x_grouped[i + 2])] + homes
+            else:
+                quantize_e(i - 1)
+                homes = [as_home(e_grouped[i - 1])] + homes
+            if len(homes) < share[i]:
+                spare = kept("spare%d" % i, [P, N], F32)
+                homes = homes + [spare[:]]
+            release(i, homes)
+            if sort_from <= i + 3 < TILES:
+                sort_words(i + 3)
             for c in interleave_at.get(i, []):
                 interleave_adj(c)
-            predict(i)
-            project(units_at.get(i, []))
-        copy_out(transpose_run(e_pairs(6)))
-        quantize_e(5)
-        weigh(7)
-        banks = [back_project(5, h) for h in range(HALVES)]
-        copy_out(transpose_run(e_pairs(7)))
+        predict(7)
+        weigh(7, 0)
+        weigh(7, 1)
         quantize_e(6)
-        release(7)
-        for h in range(HALVES):
-            finish(5, h, banks[h])
+        project(units_at[7])
+        copy_out(transpose_run(e_pairs(7)))
         project([(6, 0)])
         quantize_e(7)
         project([(6, 1), (7, 0), (7, 1)])

@@ -17,12 +17,42 @@ E2M1 = mybir.dt.float4_e2m1fn_x4
 ALU = mybir.AluOpType
 
 P = 128
-KP = 512
+SLOTS = 4
+K_PASS = P * SLOTS
+PAIRS = K_PASS // 2
 N = 512
 TILES = M // P
 PASSES = 3
 CHUNKS = F // N
 HALVES = NU // N
+ADJ_BLOCKS = HALVES * PASSES
+LAST = TILES - 1
+
+ROTATING_BANKS = 6
+STAGE_BUFS = 3
+E_LAG = 2
+UNITS_PER_ROUND = 3
+HEAD_UNITS = ((0, 0), (0, 1), (1, 0), (1, 1))
+UNITS_BEFORE_LAST_TRANSPOSES = 3
+
+
+def pieces_through(r):
+    return min(5 * (r + 1) // 2, 2 * ADJ_BLOCKS)
+
+
+def gpsimd_ops_beside(vector_ops):
+    return 2 * vector_ops // 5
+
+
+def plan_back_projections():
+    plan, done = {}, []
+    for i in range(LAST):
+        halves = range(pieces_through(i - 1) // 2 // PASSES)
+        ready = [(j, h) for j in range(i - E_LAG) for h in halves if (j, h) not in done]
+        plan[i] = ready[:UNITS_PER_ROUND]
+        done.extend(plan[i])
+    plan[LAST] = [(j, h) for j in range(TILES) for h in range(HALVES) if (j, h) not in done]
+    return plan
 
 
 def tile_condensed_mpc_update_direction_s9_kernel(
@@ -31,48 +61,55 @@ def tile_condensed_mpc_update_direction_s9_kernel(
     nc = tc.nc
     with ExitStack() as ctx:
         keep = ctx.enter_context(tc.tile_pool(name="keep", bufs=1))
-        work = ctx.enter_context(tc.tile_pool(name="work", bufs=3))
-        psum = ctx.enter_context(tc.psum_pool(name="psum", bufs=6))
-        psum_kept = ctx.enter_context(tc.psum_pool(name="psum_kept", bufs=1))
+        stage = ctx.enter_context(tc.tile_pool(name="stage", bufs=STAGE_BUFS))
+        psum = ctx.enter_context(tc.psum_pool(name="psum", bufs=ROTATING_BANKS))
+        psum_keep = ctx.enter_context(tc.psum_pool(name="psum_keep", bufs=1))
         ctx.enter_context(tc.manual_schedule())
 
         def kept(name, shape, dtype):
             return keep.tile(shape, dtype, name=name, align_bytes=64)
 
+        def kept_list(name, count, shape, dtype):
+            return [kept("%s%d" % (name, n), shape, dtype) for n in range(count)]
+
         def staged(name, shape, dtype):
-            return work.tile(shape, dtype, name=name, align_bytes=64)
+            return stage.tile(shape, dtype, name=name, align_bytes=64)
 
         def new_bank():
             return psum.tile([P, N], F32, name="bank")
 
         ident = kept("ident", [P, P], F32)
-
         phi_plane = kept("phi_plane", [P, F], U8)
         gamma_plane = kept("gamma_plane", [P, 2, F], U8)
         nc.vector.memset(phi_plane[:].bitcast(I32), 0)
         make_identity(nc, ident[:])
         nc.vector.memset(gamma_plane[:].bitcast(I32), 0)
 
-        x_sb = [kept("x%d" % j, [P, NX], BF16) for j in range(TILES)]
-        u_sb = [kept("u%d" % j, [P, NU], BF16) for j in range(TILES)]
-        y_sb = [kept("y%d" % j, [P, F], BF16) for j in range(TILES)]
+        x_sb = kept_list("x", TILES, [P, NX], BF16)
+        u_sb = kept_list("u", TILES, [P, NU], BF16)
+        y_sb = kept_list("y", TILES, [P, F], BF16)
         phi_sb = kept("phi", [P, 2 * F], U8)
         gamma_sb = kept("gamma", [P, 2, 2 * F], U8)
-        adj_sb = [kept("adj%d" % c, [P, 4, N], BF16) for c in range(HALVES * PASSES)]
-        adj_codes = [kept("adjc%d" % c, [P, N], U32) for c in range(HALVES * PASSES)]
-        adj_scales = [kept("adjs%d" % c, [P, N], U8) for c in range(HALVES * PASSES)]
-        ywt_cols = kept("ywt_cols", [P, PASSES * 4], BF16)
-        uwt_cols = kept("uwt_cols", [P, 8], BF16)
+        adj_sb = kept_list("adj", ADJ_BLOCKS, [P, SLOTS, N], BF16)
+        adj_codes = kept_list("adj_codes", ADJ_BLOCKS, [P, N], U32)
+        adj_scales = kept_list("adj_scales", ADJ_BLOCKS, [P, N], U8)
+        ywt_cols = kept("ywt_cols", [P, PASSES * SLOTS], BF16)
+        uwt_cols = kept("uwt_cols", [P, NU // P], BF16)
         uwt_rows = kept("uwt_rows", [P, NU], BF16)
-        e_codes = [kept("ec%d" % j, [P, PASSES * P], U32) for j in range(TILES)]
-        e_scales = [kept("es%d" % j, [P, PASSES * P], U8) for j in range(TILES)]
-        x_codes, x_scales, x_sorted, e_sb, adj_grouped, penalties, wide = {}, {}, {}, {}, {}, {}, {}
-        x_grouped = [kept("xg%d" % j, [P, PASSES * KP], BF16) for j in range(TILES)]
-        e_grouped = [kept("eg%d" % j, [P, PASSES * KP], BF16) for j in range(TILES)]
-        ywt_banks = [psum_kept.tile([P, N], F32, name="ywt_bank%d" % b) for b in range(2)]
+        ywt_tail = kept("ywt_tail", [P, N], BF16)
+        xu_grouped = kept_list("xu_grouped", TILES, [P, PASSES * K_PASS], BF16)
+        e_grouped = kept_list("e_grouped", TILES, [P, PASSES * K_PASS], BF16)
+        e_codes = kept_list("e_codes", TILES, [P, PASSES * P], U32)
+        e_scales = kept_list("e_scales", TILES, [P, PASSES * P], U8)
+        ywt_front_bank = psum_keep.tile([P, N], F32, name="ywt_front_bank")
+        ywt_tail_bank = psum_keep.tile([P, N], F32, name="ywt_tail_bank")
+        xu_codes, xu_scales, residual, e_sb, adj_grouped, penalties = {}, {}, {}, {}, {}, {}
 
         def rows(j):
             return slice(j * P, (j + 1) * P)
+
+        def cols_of(n, width=N):
+            return slice(n * width, (n + 1) * width)
 
         def load_xu(j):
             nc.sync.dma_start(out=x_sb[j][:], in_=x0[rows(j), :])
@@ -81,150 +118,119 @@ def tile_condensed_mpc_update_direction_s9_kernel(
         def load_y(j):
             nc.sync.dma_start(out=y_sb[j][:], in_=yref[rows(j), :])
 
-        def load_phi():
-            for r in range(4):
-                nc.sync.dma_start(out=phi_plane[r:P:32, :].bitcast(I32), in_=phi_scales[0][r:16:4, :].bitcast(I32))
-            nc.sync.dma_start(out=phi_sb[:].bitcast(I32), in_=phi_words[0].bitcast(I32))
-
-        def load_gamma():
-            nc.sync.dma_start(out=gamma_sb[:].bitcast(I32), in_=gamma_words.rearrange("g p b -> p g b").bitcast(I32))
-            for r in range(4):
-                src = gamma_scales.rearrange("g q n -> q g n")[r:16:4, :, :]
-                nc.sync.dma_start(out=gamma_plane[r:P:32, :, :].bitcast(I32), in_=src.bitcast(I32))
-
-        def load_ywt():
-            src = ywt.rearrange("(g q e) -> q g e", q=P, e=4)
-            nc.sync.dma_start(out=ywt_cols[:].rearrange("q (g e) -> q g e", e=4), in_=src)
-
-        def load_uwt():
-            nc.sync.dma_start(out=uwt_cols[:], in_=uwt.rearrange("(n e) -> n e", e=8))
-
-        def load_adj(c):
-            h, g = divmod(c, PASSES)
-            src = adj[g * KP : (g + 1) * KP, h * N : (h + 1) * N].rearrange("(p t) n -> p t n", t=4)
-            nc.sync.dma_start(out=adj_sb[c][:], in_=src)
+        def load_adj(block):
+            h, g = divmod(block, PASSES)
+            src = adj[cols_of(g, K_PASS), cols_of(h)].rearrange("(p t) n -> p t n", t=SLOTS)
+            nc.sync.dma_start(out=adj_sb[block][:], in_=src)
 
         load_xu(0)
-        load_phi()
-        load_ywt()
-        load_gamma()
+        for r in range(4):
+            nc.sync.dma_start(out=phi_plane[r:P:32, :].bitcast(I32), in_=phi_scales[0][r:16:4, :].bitcast(I32))
+        nc.sync.dma_start(out=phi_sb[:].bitcast(I32), in_=phi_words[0].bitcast(I32))
+        nc.sync.dma_start(out=uwt_cols[:], in_=uwt.rearrange("(n e) -> n e", n=P))
+        nc.sync.dma_start(out=gamma_sb[:].bitcast(I32), in_=gamma_words.rearrange("g p b -> p g b").bitcast(I32))
+        for r in range(4):
+            src = gamma_scales.rearrange("g q n -> q g n")[r:16:4, :, :]
+            nc.sync.dma_start(out=gamma_plane[r:P:32, :, :].bitcast(I32), in_=src.bitcast(I32))
         load_xu(1)
         load_y(0)
-        load_uwt()
+        nc.sync.dma_start(
+            out=ywt_cols[:].rearrange("p (g t) -> p g t", t=SLOTS), in_=ywt.rearrange("(g p t) -> p g t", p=P, t=SLOTS)
+        )
         load_adj(0)
         load_xu(2)
         load_y(1)
         load_adj(1)
-        for j in range(2, 6):
-            load_xu(j + 1)
-            load_adj(j)
+        for j in range(2, TILES):
+            if j < LAST:
+                load_xu(j + 1)
+            if j < ADJ_BLOCKS:
+                load_adj(j)
             load_y(j)
-        load_xu(7)
-        load_y(6)
-        load_y(7)
 
-        def x_pairs(j):
-            xw = x_sb[j][:].bitcast(F32)
-            uw = u_sb[j][:].bitcast(F32)
-            srcs = [[xw[:, w:256:2] for w in range(2)]]
-            srcs += [[uw[:, 256 * g + w : 256 * (g + 1) : 2] for w in range(2)] for g in range(2)]
-            if j in x_sorted:
-                srcs = [[x_sorted[j][:, 256 * g + P * w : 256 * g + P * (w + 1)] for w in range(2)] for g in range(PASSES)]
-            return [(srcs[g], x_grouped[j], g, True) for g in range(PASSES)]
+        def xu_passes(j):
+            x_words = x_sb[j][:].bitcast(F32)
+            u_words = u_sb[j][:].bitcast(F32)
+            sources = [[x_words[:, w:PAIRS:2] for w in range(2)]]
+            sources.extend([u_words[:, PAIRS * g + w : PAIRS * (g + 1) : 2] for w in range(2)] for g in range(2))
+            return [(sources[g], xu_grouped[j], g) for g in range(PASSES)]
 
-        def e_pairs(j):
-            ew = e_sb[j][:].bitcast(F32)
-            return [([ew[:, 256 * g + P * w : 256 * g + P * (w + 1)] for w in range(2)], e_grouped[j], g, True) for g in range(PASSES)]
+        def e_passes(j):
+            e_words = e_sb[j][:].bitcast(F32)
+            return [([e_words[:, cols_of(2 * g + w, P)] for w in range(2)], e_grouped[j], g) for g in range(PASSES)]
 
-        def spread_ywt():
-            cols = ywt_cols[:].bitcast(F32)
-            for c in range(2 * PASSES):
-                nc.tensor.transpose(ywt_banks[c // 4][:, P * (c % 4) : P * (c % 4 + 1)], cols[:, c : c + 1].to_broadcast([P, P]), ident[:])
-
-        def sort_words(j):
-            x_sorted[j] = staged("x_sorted", [P, PASSES * 256], F32)
-            nc.scalar.copy(
-                out=x_sorted[j][:, :256].rearrange("p (w q) -> p w q", w=2),
-                in_=x_sb[j][:].bitcast(F32).rearrange("p (q w) -> p w q", w=2),
-            )
-            nc.scalar.copy(
-                out=x_sorted[j][:, 256:].rearrange("p (g w q) -> p g w q", g=2, w=2),
-                in_=u_sb[j][:].bitcast(F32).rearrange("p (g q w) -> p g w q", g=2, w=2),
-            )
-
-        def transpose_run(pairs):
+        def transpose_and_group(passes):
             copies = []
-            for b in range(0, len(pairs), 2):
+            for first in range(0, len(passes), 2):
                 bank = new_bank()
-                group = pairs[b : b + 2]
-                for s, pair in enumerate(group):
+                in_bank = passes[first : first + 2]
+                for s, (sources, grouped, g) in enumerate(in_bank):
                     for w in range(2):
-                        nc.tensor.transpose(bank[:, 256 * s + P * w : 256 * s + P * (w + 1)], pair[0][w], ident[:])
-                if len(group) == 2 and group[0][1] is group[1][1]:
-                    copies.append((bank, 0, 2, group[0]))
+                        nc.tensor.transpose(bank[:, cols_of(2 * s + w, P)], sources[w], ident[:])
+                if len(in_bank) == 2 and in_bank[0][1] is in_bank[1][1]:
+                    copies.append((bank[:], in_bank[0][1], in_bank[0][2], 2))
                 else:
-                    copies.extend((bank, s, 1, pair) for s, pair in enumerate(group))
-            return copies
+                    copies.extend((bank[:, cols_of(s, PAIRS)], grouped, g, 1) for s, (sources, grouped, g) in enumerate(in_bank))
+            for src, grouped, g, count in copies:
+                dst = grouped[:].bitcast(F32)[:, PAIRS * g : PAIRS * (g + count)]
+                nc.scalar.copy(
+                    out=dst.rearrange("p (g m w) -> p g m w", w=2, m=P), in_=src.rearrange("p (g w m) -> p g m w", w=2, m=P)
+                )
 
-        def copy_out(copies):
-            for bank, s, count, (srcs, dst, g, interleave) in copies:
-                src = bank[:, 256 * s : 256 * (s + count)]
-                words = dst[:].bitcast(F32)[:, 256 * g : 256 * (g + count)]
-                if interleave:
-                    nc.scalar.copy(
-                        out=words.rearrange("p (g r w) -> p g r w", w=2, r=P), in_=src.rearrange("p (g w r) -> p g r w", w=2, r=P)
-                    )
-                else:
-                    nc.scalar.copy(out=words, in_=src)
+        def spread(bank, at, column):
+            nc.tensor.transpose(bank[:, cols_of(at, P)], column.to_broadcast([P, P]), ident[:])
 
         def spread_uwt():
             bank = new_bank()
-            cols = uwt_cols[:].bitcast(F32)
+            words = uwt_cols[:].bitcast(F32)
             for c in range(4):
-                nc.tensor.transpose(bank[:, P * c : P * (c + 1)], cols[:, c : c + 1].to_broadcast([P, P]), ident[:])
-            return bank
-
-        def copy_uwt(bank):
+                spread(bank, c, words[:, c : c + 1])
             nc.scalar.copy(
                 out=uwt_rows[:].bitcast(F32).rearrange("p (n c) -> p n c", c=4), in_=bank[:].rearrange("p (c n) -> p n c", c=4)
             )
 
-        def quantize(codes, scales, grouped, fmt, spans):
-            for a, b in spans:
+        def spread_ywt():
+            words = ywt_cols[:].bitcast(F32)
+            for c in range(2 * PASSES):
+                spread(ywt_front_bank if c < 4 else ywt_tail_bank, c % 4, words[:, c : c + 1])
+
+        def quantize(codes, scales, grouped, fmt, split):
+            for a, b in ((0, split), (split, PASSES)):
                 nc.vector.quantize_mx(
-                    out=codes[:, P * a : P * b].bitcast(fmt), scales=scales[:, P * a : P * b], in_=grouped[:, KP * a : KP * b]
+                    out=codes[:, P * a : P * b].bitcast(fmt), scales=scales[:, P * a : P * b], in_=grouped[:, K_PASS * a : K_PASS * b]
                 )
 
-        def quantize_x(j, spans=((0, 2), (2, 3))):
-            x_codes[j] = staged("x_codes", [P, PASSES * P], U32)
-            x_scales[j] = staged("x_scales", [P, PASSES * P], U8)
-            quantize(x_codes[j], x_scales[j], x_grouped[j], E4M3, spans)
+        def quantize_xu(j, split=2):
+            xu_codes[j] = staged("xu_codes", [P, PASSES * P], U32)
+            xu_scales[j] = staged("xu_scales", [P, PASSES * P], U8)
+            quantize(xu_codes[j], xu_scales[j], xu_grouped[j], E4M3, split)
 
         def quantize_e(j):
-            quantize(e_codes[j], e_scales[j], e_grouped[j], E5M2, [(0, 1), (1, 3)])
+            quantize(e_codes[j], e_scales[j], e_grouped[j], E5M2, 1)
 
-        def interleave_adj(piece):
-            c, part = divmod(piece, 2)
-            if part == 0:
-                adj_grouped[c] = staged("adj_grouped", [P, 4 * N], BF16)
-            cols = slice(part * N // 2, (part + 1) * N // 2)
-            nc.scalar.copy(
-                out=adj_grouped[c][:, 2 * N * part : 2 * N * (part + 1)].rearrange("p (c i t) -> p c t i", i=4, t=4),
-                in_=adj_sb[c][:, :, cols].rearrange("p t (c i) -> p c t i", i=4),
-            )
+        def interleave_adj(r):
+            for piece in range(pieces_through(r - 1), pieces_through(r)):
+                block, part = divmod(piece, 2)
+                if part == 0:
+                    adj_grouped[block] = staged("adj_grouped", [P, SLOTS * N], BF16)
+                nc.scalar.copy(
+                    out=adj_grouped[block][:, cols_of(part, 2 * N)].rearrange("p (c i t) -> p c t i", i=4, t=SLOTS),
+                    in_=adj_sb[block][:, :, cols_of(part, N // 2)].rearrange("p t (c i) -> p c t i", i=4),
+                )
 
-        def quantize_adj(c):
-            nc.vector.quantize_mx(out=adj_codes[c][:].bitcast(E4M3), scales=adj_scales[c][:], in_=adj_grouped[c][:])
+        def quantize_adj(r):
+            for block in range(pieces_through(r - 1) // 2, pieces_through(r) // 2):
+                nc.vector.quantize_mx(
+                    out=adj_codes[block][:].bitcast(E4M3), scales=adj_scales[block][:], in_=adj_grouped[block][:]
+                )
 
         def predict_pass(bank, j, n, g):
-            cols = slice(n * N, (n + 1) * N)
-            byte_cols = slice(2 * N * n, 2 * N * (n + 1))
-            words = phi_sb[:, byte_cols] if g == 0 else gamma_sb[:, g - 1, byte_cols]
-            plane = phi_plane[:, cols] if g == 0 else gamma_plane[:, g - 1, cols]
+            words = phi_sb[:, cols_of(n, 2 * N)] if g == 0 else gamma_sb[:, g - 1, cols_of(n, 2 * N)]
+            plane = phi_plane[:, cols_of(n)] if g == 0 else gamma_plane[:, g - 1, cols_of(n)]
             nc.tensor.matmul_mx(
                 out=bank[:],
-                lhsT=x_codes[j][:, P * g : P * (g + 1)].bitcast(E4M3),
-                lhsT_scale=x_scales[j][:, P * g : P * (g + 1)],
+                lhsT=xu_codes[j][:, cols_of(g, P)].bitcast(E4M3),
+                lhsT_scale=xu_scales[j][:, cols_of(g, P)],
                 rhs=words.bitcast(E2M1),
                 rhs_scale=plane,
                 start=(g == 0),
@@ -233,138 +239,148 @@ def tile_condensed_mpc_update_direction_s9_kernel(
 
         def subtract_reference(bank, j, n):
             if n == 0:
-                wide[j] = staged("wide", [P, F], F32)
-            cols = slice(n * N, (n + 1) * N)
+                residual[j] = staged("residual", [P, F], F32)
+                e_sb[j] = staged("e_sb", [P, F], BF16)
             nc.vector.tensor_tensor(
-                out=wide[j][:, cols].rearrange("p (w q b) -> p w q b", w=2, b=2),
-                in0=bank[:].rearrange("p (q w b) -> p w q b", w=2, b=2),
-                in1=y_sb[j][:, cols].rearrange("p (q w b) -> p w q b", w=2, b=2),
+                out=residual[j][:, cols_of(n)].rearrange("m (w p b) -> m w p b", w=2, b=2),
+                in0=bank[:].rearrange("m (p w b) -> m w p b", w=2, b=2),
+                in1=y_sb[j][:, cols_of(n)].rearrange("m (p w b) -> m w p b", w=2, b=2),
                 op=ALU.subtract,
             )
 
-        def predict(j, chunks=range(CHUNKS)):
+        def predict(j, chunks):
             for n in chunks:
                 bank = new_bank()
                 for g in range(PASSES):
                     predict_pass(bank, j, n, g)
                 subtract_reference(bank, j, n)
 
-        def weigh(j, b):
-            if b == 0:
-                e_sb[j] = staged("e_sb", [P, F], BF16)
-            cols = slice(2 * N * b, min(2 * N * (b + 1), F))
-            weights = ywt_banks[b][:].bitcast(BF16)[:, : cols.stop - cols.start]
-            nc.vector.tensor_tensor(out=e_sb[j][:, cols], in0=wide[j][:, cols], in1=weights, op=ALU.mult)
+        plan = plan_back_projections()
+        penalty_queue = [unit for i in range(TILES) for unit in plan[i] if unit not in HEAD_UNITS]
+        gpsimd_weighs = [i for i in range(LAST) if plan[i]]
+        deferred = []
 
-        def penalty(engine, unit, home):
+        def penalty(unit, quantised=None):
             j, h = unit
-            cols = slice(h * N, (h + 1) * N)
-            penalties[unit] = home
-            engine.tensor_tensor(out=home, in0=u_sb[j][:, cols], in1=uwt_rows[:, cols], op=ALU.mult)
+            if quantised is None:
+                own = kept("penalty%d_%d" % unit, [P, N], F32)
+                penalties[unit] = own[:]
+            else:
+                penalties[unit] = quantised[:].bitcast(F32)[:, N // 2 :]
+            nc.gpsimd.tensor_tensor(out=penalties[unit], in0=u_sb[j][:, cols_of(h)], in1=uwt_rows[:, cols_of(h)], op=ALU.mult)
 
-        def back_project(j, h):
-            bank = new_bank()
-            for g in range(PASSES):
-                nc.tensor.matmul_mx(
-                    out=bank[:],
-                    lhsT=e_codes[j][:, P * g : P * (g + 1)].bitcast(E5M2),
-                    lhsT_scale=e_scales[j][:, P * g : P * (g + 1)],
-                    rhs=adj_codes[PASSES * h + g][:].bitcast(E4M3),
-                    rhs_scale=adj_scales[PASSES * h + g][:],
-                    start=(g == 0),
-                    stop=(g == PASSES - 1),
+        def start_penalties(count, quantised):
+            batch = penalty_queue[:count]
+            for unit in batch:
+                penalty_queue.remove(unit)
+            penalty(batch[0], quantised)
+            deferred.extend(batch[1:])
+
+        def penalties_beside(i):
+            if i == LAST:
+                return len(penalty_queue)
+            handed_over = 1 if i in gpsimd_weighs else 0
+            return gpsimd_ops_beside(2 * CHUNKS - handed_over + len(plan[i])) - handed_over
+
+        def weigh(j):
+            front, tail = slice(0, 2 * N), slice(2 * N, F)
+            if j in gpsimd_weighs:
+                nc.gpsimd.tensor_tensor(out=e_sb[j][:, tail], in0=residual[j][:, tail], in1=ywt_tail[:], op=ALU.mult)
+            for unit in deferred:
+                penalty(unit)
+            deferred.clear()
+            nc.vector.tensor_tensor(
+                out=e_sb[j][:, front], in0=residual[j][:, front], in1=ywt_front_bank[:].bitcast(BF16), op=ALU.mult
+            )
+            if j not in gpsimd_weighs:
+                nc.vector.tensor_tensor(
+                    out=e_sb[j][:, tail], in0=residual[j][:, tail], in1=ywt_tail_bank[:].bitcast(BF16)[:, :N], op=ALU.mult
                 )
-            return bank
 
-        def finish(j, h, bank):
-            home = penalties[(j, h)]
-            nc.vector.tensor_tensor(out=home, in0=bank[:], in1=home, op=ALU.add)
-            nc.sync.dma_start(out=out[rows(j), h * N : (h + 1) * N], in_=home)
-
-        interleave_at = {-1: [0, 1], 0: [2, 3, 4], 1: [5, 6, 7], 2: [8, 9, 10], 3: [11]}
-        quantize_at = {0: [0], 1: [1], 2: [2], 3: [3, 4], 4: [5]}
-        units_at = {3: [(0, 0)], 4: [(1, 0)], 5: [(2, 0), (0, 1), (1, 1)], 6: [(3, 0), (2, 1), (3, 1)], 7: [(4, 0), (4, 1), (5, 0), (5, 1)]}
-        order = [x for i in sorted(units_at) for x in units_at[i]]
-        order = order + [(j, h) for j in range(TILES) for h in range(HALVES) if (j, h) not in order]
-        share = [1, 2, 3, 2, 3, 3, 2, 0]
-        sort_from = 9
-
-        def release(i, homes):
-            first = sum(share[:i])
-            for s in range(share[i]):
-                penalty(nc.gpsimd, order[first + s], homes[s])
-
-        def as_home(grouped):
-            return grouped[:].bitcast(F32)[:, N // 2 :]
-
-        def project(units):
+        def back_project(units):
             for j, h in units:
-                finish(j, h, back_project(j, h))
+                bank = new_bank()
+                for g in range(PASSES):
+                    nc.tensor.matmul_mx(
+                        out=bank[:],
+                        lhsT=e_codes[j][:, cols_of(g, P)].bitcast(E5M2),
+                        lhsT_scale=e_scales[j][:, cols_of(g, P)],
+                        rhs=adj_codes[PASSES * h + g][:].bitcast(E4M3),
+                        rhs_scale=adj_scales[PASSES * h + g][:],
+                        start=(g == 0),
+                        stop=(g == PASSES - 1),
+                    )
+                parts = 2 if (j, h) == (LAST, HALVES - 1) else 1
+                for part in range(parts):
+                    cols = cols_of(part, N // parts)
+                    result = penalties[(j, h)][:, cols]
+                    nc.vector.tensor_tensor(out=result, in0=bank[:, cols], in1=result, op=ALU.add)
+                    nc.sync.dma_start(out=out[rows(j), cols_of(h)][:, cols], in_=result)
 
-        first_pairs = x_pairs(0)
-        copy_out(transpose_run(first_pairs[:1]) + transpose_run(first_pairs[1:]))
-        quantize_x(0, ((0, 1), (1, 3)))
+        first_passes = xu_passes(0)
+        transpose_and_group(first_passes[:1])
+        transpose_and_group(first_passes[1:])
+        spread_uwt()
+        quantize_xu(0, split=1)
+        penalty(HEAD_UNITS[0], xu_grouped[0])
+        penalty(HEAD_UNITS[1])
         banks = [new_bank() for n in range(CHUNKS)]
         for n in range(CHUNKS):
             predict_pass(banks[n], 0, n, 0)
-        for n in range(CHUNKS):
+
+        def finish_first_tile(n):
             for g in range(1, PASSES):
                 predict_pass(banks[n], 0, n, g)
             subtract_reference(banks[n], 0, n)
-            if n == 0:
-                copy_out(transpose_run(x_pairs(1)))
-            if n == 1:
-                quantize_x(1)
+
+        finish_first_tile(0)
+        transpose_and_group(xu_passes(1))
+        finish_first_tile(1)
+        quantize_xu(1)
+        penalty(HEAD_UNITS[2], xu_grouped[1])
+        penalty(HEAD_UNITS[3])
+        finish_first_tile(2)
         spread_ywt()
-        for c in interleave_at[-1]:
-            interleave_adj(c)
-        copy_uwt(spread_uwt())
-        weigh(0, 0)
-        weigh(0, 1)
+        interleave_adj(0)
+        weigh(0)
+
         predict(1, [0])
-        copy_out(transpose_run(x_pairs(2)))
-        for c in interleave_at.get(0, []):
-            interleave_adj(c)
+        transpose_and_group(xu_passes(2))
+        interleave_adj(1)
         predict(1, [1])
-        for c in quantize_at.get(0, []):
-            quantize_adj(c)
-        quantize_x(2)
-        release(0, [as_home(x_grouped[2]), as_home(x_grouped[1])])
+        quantize_adj(0)
+        quantize_xu(2)
+        start_penalties(gpsimd_ops_beside(1 + CHUNKS), xu_grouped[2])
         predict(1, [2])
-        for i in range(1, TILES - 1):
+
+        for i in range(1, LAST):
             if i > 1:
-                predict(i)
-            weigh(i, 0)
-            weigh(i, 1)
-            project(units_at.get(i, []))
-            pairs = x_pairs(i + 2) + e_pairs(i - 1) if i + 2 < TILES else e_pairs(i - 1) + e_pairs(i)
-            copy_out(transpose_run(pairs))
-            homes = []
-            for c in quantize_at.get(i, []):
-                quantize_adj(c)
-            if i >= 2:
-                quantize_e(i - 2)
-                homes = [as_home(e_grouped[i - 2])] + homes
-            if i + 2 < TILES:
-                quantize_x(i + 2)
-                homes = [as_home(x_grouped[i + 2])] + homes
+                predict(i, range(CHUNKS))
+            weigh(i)
+            back_project(plan[i])
+            ahead = i + 2
+            if ahead < TILES:
+                transpose_and_group(xu_passes(ahead) + e_passes(i - 1))
+            else:
+                transpose_and_group(e_passes(i - 1) + e_passes(i))
+            quantize_adj(i)
+            if i >= E_LAG:
+                quantize_e(i - E_LAG)
+            if ahead < TILES:
+                quantize_xu(ahead)
+                start_penalties(penalties_beside(i + 1), xu_grouped[ahead])
             else:
                 quantize_e(i - 1)
-                homes = [as_home(e_grouped[i - 1])] + homes
-            if len(homes) < share[i]:
-                spare = kept("spare%d" % i, [P, N], F32)
-                homes = homes + [spare[:]]
-            release(i, homes)
-            if sort_from <= i + 3 < TILES:
-                sort_words(i + 3)
-            for c in interleave_at.get(i, []):
-                interleave_adj(c)
-        predict(7)
-        weigh(7, 0)
-        weigh(7, 1)
-        quantize_e(6)
-        project(units_at[7])
-        copy_out(transpose_run(e_pairs(7)))
-        project([(6, 0)])
-        quantize_e(7)
-        project([(6, 1), (7, 0), (7, 1)])
+                start_penalties(penalties_beside(i + 1), e_grouped[i - 1])
+            if i == 1:
+                nc.scalar.copy(out=ywt_tail[:].bitcast(F32), in_=ywt_tail_bank[:, :PAIRS])
+            interleave_adj(i + 1)
+
+        predict(LAST, range(CHUNKS))
+        weigh(LAST)
+        quantize_e(LAST - 1)
+        back_project(plan[LAST][:UNITS_BEFORE_LAST_TRANSPOSES])
+        transpose_and_group(e_passes(LAST))
+        back_project(plan[LAST][UNITS_BEFORE_LAST_TRANSPOSES : UNITS_BEFORE_LAST_TRANSPOSES + 1])
+        quantize_e(LAST)
+        back_project(plan[LAST][UNITS_BEFORE_LAST_TRANSPOSES + 1 :])

@@ -31,13 +31,9 @@ LAST = TILES - 1
 ROTATING_BANKS = 6
 STAGE_BUFS = 3
 E_LAG = 2
-UNITS_PER_ROUND = 3
+UNITS_PER_ROUND = 4
 HEAD_UNITS = ((0, 0), (0, 1), (1, 0), (1, 1))
 UNITS_BEFORE_LAST_TRANSPOSES = 3
-
-
-def pieces_through(r):
-    return min(5 * (r + 1) // 2, 2 * ADJ_BLOCKS)
 
 
 def gpsimd_ops_beside(vector_ops):
@@ -47,7 +43,7 @@ def gpsimd_ops_beside(vector_ops):
 def plan_back_projections():
     plan, done = {}, []
     for i in range(LAST):
-        halves = range(pieces_through(i - 1) // 2 // PASSES)
+        halves = range(i // PASSES)
         ready = [(j, h) for j in range(i - E_LAG) for h in halves if (j, h) not in done]
         plan[i] = ready[:UNITS_PER_ROUND]
         done.extend(plan[i])
@@ -208,21 +204,14 @@ def tile_condensed_mpc_update_direction_s9_kernel(
         def quantize_e(j):
             quantize(e_codes[j], e_scales[j], e_grouped[j], E5M2, 1)
 
-        def interleave_adj(r):
-            for piece in range(pieces_through(r - 1), pieces_through(r)):
-                block, part = divmod(piece, 2)
-                if part == 0:
-                    adj_grouped[block] = staged("adj_grouped", [P, SLOTS * N], BF16)
-                nc.scalar.copy(
-                    out=adj_grouped[block][:, cols_of(part, 2 * N)].rearrange("p (c i t) -> p c t i", i=4, t=SLOTS),
-                    in_=adj_sb[block][:, :, cols_of(part, N // 2)].rearrange("p t (c i) -> p c t i", i=4),
-                )
+        def interleave_adj(block):
+            adj_grouped[block] = staged("adj_grouped", [P, SLOTS * N], BF16)
+            nc.scalar.copy(
+                out=adj_grouped[block][:].rearrange("p (n t) -> p n t", t=SLOTS), in_=adj_sb[block][:].rearrange("p t n -> p n t")
+            )
 
-        def quantize_adj(r):
-            for block in range(pieces_through(r - 1) // 2, pieces_through(r) // 2):
-                nc.vector.quantize_mx(
-                    out=adj_codes[block][:].bitcast(E4M3), scales=adj_scales[block][:], in_=adj_grouped[block][:]
-                )
+        def quantize_adj(block):
+            nc.vector.quantize_mx(out=adj_codes[block][:].bitcast(E4M3), scales=adj_scales[block][:], in_=adj_grouped[block][:])
 
         def predict_pass(bank, j, n, g):
             words = phi_sb[:, cols_of(n, 2 * N)] if g == 0 else gamma_sb[:, g - 1, cols_of(n, 2 * N)]
@@ -363,7 +352,8 @@ def tile_condensed_mpc_update_direction_s9_kernel(
                 transpose_and_group(xu_passes(ahead) + e_passes(i - 1))
             else:
                 transpose_and_group(e_passes(i - 1) + e_passes(i))
-            quantize_adj(i)
+            if i < ADJ_BLOCKS:
+                quantize_adj(i)
             if i >= E_LAG:
                 quantize_e(i - E_LAG)
             if ahead < TILES:
@@ -374,7 +364,8 @@ def tile_condensed_mpc_update_direction_s9_kernel(
                 start_penalties(penalties_beside(i + 1), e_grouped[i - 1])
             if i == 1:
                 nc.scalar.copy(out=ywt_tail[:].bitcast(F32), in_=ywt_tail_bank[:, :PAIRS])
-            interleave_adj(i + 1)
+            if i + 1 < ADJ_BLOCKS:
+                interleave_adj(i + 1)
 
         predict(LAST, range(CHUNKS))
         weigh(LAST)

from contextlib import ExitStack

import concourse.mybir as mybir
from concourse.masks import make_identity

M, NX, NU, F = 1024, 512, 1024, 1536
FLOPS = 2 * M * (NX + NU) * F + 2 * M * F * NU

F32 = mybir.dt.float32
BF16 = mybir.dt.bfloat16
I32 = mybir.dt.int32
U32 = mybir.dt.uint32
U8 = mybir.dt.uint8
E4M3 = mybir.dt.float8_e4m3fn_x4
E5M2 = mybir.dt.float8_e5m2_x4
E2M1 = mybir.dt.float4_e2m1fn_x4
ALU = mybir.AluOpType

P = 128
SLOTS = 4
K_PASS = P * SLOTS
PAIRS = K_PASS // 2
N = 512
TILES = M // P
PASSES = 3
CHUNKS = F // N
HALVES = NU // N
ADJ_BLOCKS = HALVES * PASSES
LAST = TILES - 1

ROTATING_BANKS = 6
STAGE_BUFS = 3
E_LAG = 2
UNITS_PER_ROUND = 4
HEAD_UNITS = ((0, 0), (0, 1), (1, 0), (1, 1))
UNITS_BEFORE_LAST_TRANSPOSES = 3


def gpsimd_ops_beside(vector_ops):
    return 2 * vector_ops // 5


def plan_back_projections():
    plan, done = {}, []
    for i in range(LAST):
        halves = range(i // PASSES)
        ready = [(j, h) for j in range(i - E_LAG) for h in halves if (j, h) not in done]
        plan[i] = ready[:UNITS_PER_ROUND]
        done.extend(plan[i])
    plan[LAST] = [(j, h) for j in range(TILES) for h in range(HALVES) if (j, h) not in done]
    return plan


def tile_condensed_mpc_update_direction_s9_kernel(
    tc, x0, u, phi_words, phi_scales, gamma_words, gamma_scales, yref, ywt, adj, uwt, out
):
    nc = tc.nc
    with ExitStack() as ctx:
        keep = ctx.enter_context(tc.tile_pool(name="keep", bufs=1))
        stage = ctx.enter_context(tc.tile_pool(name="stage", bufs=STAGE_BUFS))
        psum = ctx.enter_context(tc.psum_pool(name="psum", bufs=ROTATING_BANKS))
        psum_keep = ctx.enter_context(tc.psum_pool(name="psum_keep", bufs=1))
        ctx.enter_context(tc.manual_schedule())

        def kept(name, shape, dtype):
            return keep.tile(shape, dtype, name=name, align_bytes=64)

        def kept_list(name, count, shape, dtype):
            return [kept("%s%d" % (name, n), shape, dtype) for n in range(count)]

        def staged(name, shape, dtype):
            return stage.tile(shape, dtype, name=name, align_bytes=64)

        def new_bank():
            return psum.tile([P, N], F32, name="bank")

        ident = kept("ident", [P, P], F32)
        phi_plane = kept("phi_plane", [P, F], U8)
        gamma_plane = kept("gamma_plane", [P, 2, F], U8)
        nc.vector.memset(phi_plane[:].bitcast(I32), 0)
        make_identity(nc, ident[:])
        nc.vector.memset(gamma_plane[:].bitcast(I32), 0)

        x_sb = kept_list("x", TILES, [P, NX], BF16)
        u_sb = kept_list("u", TILES, [P, NU], BF16)
        y_sb = kept_list("y", TILES, [P, F], BF16)
        phi_sb = kept("phi", [P, 2 * F], U8)
        gamma_sb = kept("gamma", [P, 2, 2 * F], U8)
        adj_sb = kept_list("adj", ADJ_BLOCKS, [P, SLOTS, N], BF16)
        adj_codes = kept_list("adj_codes", ADJ_BLOCKS, [P, N], U32)
        adj_scales = kept_list("adj_scales", ADJ_BLOCKS, [P, N], U8)
        ywt_cols = kept("ywt_cols", [P, PASSES * SLOTS], BF16)
        uwt_cols = kept("uwt_cols", [P, NU // P], BF16)
        uwt_rows = kept("uwt_rows", [P, NU], BF16)
        ywt_tail = kept("ywt_tail", [P, N], BF16)
        xu_grouped = kept_list("xu_grouped", TILES, [P, PASSES * K_PASS], BF16)
        e_grouped = kept_list("e_grouped", TILES, [P, PASSES * K_PASS], BF16)
        e_codes = kept_list("e_codes", TILES, [P, PASSES * P], U32)
        e_scales = kept_list("e_scales", TILES, [P, PASSES * P], U8)
        ywt_front_bank = psum_keep.tile([P, N], F32, name="ywt_front_bank")
        ywt_tail_bank = psum_keep.tile([P, N], F32, name="ywt_tail_bank")
        xu_codes, xu_scales, residual, e_sb, adj_grouped, penalties = {}, {}, {}, {}, {}, {}

        def rows(j):
            return slice(j * P, (j + 1) * P)

        def cols_of(n, width=N):
            return slice(n * width, (n + 1) * width)

        def load_xu(j):
            nc.sync.dma_start(out=x_sb[j][:], in_=x0[rows(j), :])
            nc.sync.dma_start(out=u_sb[j][:], in_=u[rows(j), :])

        def load_y(j):
            nc.sync.dma_start(out=y_sb[j][:], in_=yref[rows(j), :])

        def load_adj(block):
            h, g = divmod(block, PASSES)
            src = adj[cols_of(g, K_PASS), cols_of(h)].rearrange("(p t) n -> p t n", t=SLOTS)
            nc.sync.dma_start(out=adj_sb[block][:], in_=src)

        load_xu(0)
        for r in range(4):
            nc.sync.dma_start(out=phi_plane[r:P:32, :].bitcast(I32), in_=phi_scales[0][r:16:4, :].bitcast(I32))
        nc.sync.dma_start(out=phi_sb[:].bitcast(I32), in_=phi_words[0].bitcast(I32))
        nc.sync.dma_start(out=uwt_cols[:], in_=uwt.rearrange("(n e) -> n e", n=P))
        nc.sync.dma_start(out=gamma_sb[:].bitcast(I32), in_=gamma_words.rearrange("g p b -> p g b").bitcast(I32))
        for r in range(4):
            src = gamma_scales.rearrange("g q n -> q g n")[r:16:4, :, :]
            nc.sync.dma_start(out=gamma_plane[r:P:32, :, :].bitcast(I32), in_=src.bitcast(I32))
        load_xu(1)
        load_y(0)
        nc.sync.dma_start(
            out=ywt_cols[:].rearrange("p (g t) -> p g t", t=SLOTS), in_=ywt.rearrange("(g p t) -> p g t", p=P, t=SLOTS)
        )
        load_adj(0)
        load_xu(2)
        load_y(1)
        load_adj(1)
        for j in range(2, TILES):
            if j < LAST:
                load_xu(j + 1)
            if j < ADJ_BLOCKS:
                load_adj(j)
            load_y(j)

        def xu_passes(j):
            x_words = x_sb[j][:].bitcast(F32)
            u_words = u_sb[j][:].bitcast(F32)
            sources = [[x_words[:, w:PAIRS:2] for w in range(2)]]
            sources.extend([u_words[:, PAIRS * g + w : PAIRS * (g + 1) : 2] for w in range(2)] for g in range(2))
            return [(sources[g], xu_grouped[j], g) for g in range(PASSES)]

        def e_passes(j):
            e_words = e_sb[j][:].bitcast(F32)
            return [([e_words[:, cols_of(2 * g + w, P)] for w in range(2)], e_grouped[j], g) for g in range(PASSES)]

        def transpose_and_group(passes):
            copies = []
            for first in range(0, len(passes), 2):
                bank = new_bank()
                in_bank = passes[first : first + 2]
                for s, (sources, grouped, g) in enumerate(in_bank):
                    for w in range(2):
                        nc.tensor.transpose(bank[:, cols_of(2 * s + w, P)], sources[w], ident[:])
                if len(in_bank) == 2 and in_bank[0][1] is in_bank[1][1]:
                    copies.append((bank[:], in_bank[0][1], in_bank[0][2], 2))
                else:
                    copies.extend((bank[:, cols_of(s, PAIRS)], grouped, g, 1) for s, (sources, grouped, g) in enumerate(in_bank))
            for src, grouped, g, count in copies:
                dst = grouped[:].bitcast(F32)[:, PAIRS * g : PAIRS * (g + count)]
                nc.scalar.copy(
                    out=dst.rearrange("p (g m w) -> p g m w", w=2, m=P), in_=src.rearrange("p (g w m) -> p g m w", w=2, m=P)
                )

        def spread(bank, at, column):
            nc.tensor.transpose(bank[:, cols_of(at, P)], column.to_broadcast([P, P]), ident[:])

        def spread_uwt():
            bank = new_bank()
            words = uwt_cols[:].bitcast(F32)
            for c in range(4):
                spread(bank, c, words[:, c : c + 1])
            nc.scalar.copy(
                out=uwt_rows[:].bitcast(F32).rearrange("p (n c) -> p n c", c=4), in_=bank[:].rearrange("p (c n) -> p n c", c=4)
            )

        def spread_ywt():
            words = ywt_cols[:].bitcast(F32)
            for c in range(2 * PASSES):
                spread(ywt_front_bank if c < 4 else ywt_tail_bank, c % 4, words[:, c : c + 1])

        def quantize(codes, scales, grouped, fmt, split):
            for a, b in ((0, split), (split, PASSES)):
                nc.vector.quantize_mx(
                    out=codes[:, P * a : P * b].bitcast(fmt), scales=scales[:, P * a : P * b], in_=grouped[:, K_PASS * a : K_PASS * b]
                )

        def quantize_xu(j, split=2):
            xu_codes[j] = staged("xu_codes", [P, PASSES * P], U32)
            xu_scales[j] = staged("xu_scales", [P, PASSES * P], U8)
            quantize(xu_codes[j], xu_scales[j], xu_grouped[j], E4M3, split)

        def quantize_e(j):
            quantize(e_codes[j], e_scales[j], e_grouped[j], E5M2, 1)

        def interleave_adj(block):
            adj_grouped[block] = staged("adj_grouped", [P, SLOTS * N], BF16)
            nc.scalar.copy(
                out=adj_grouped[block][:].rearrange("p (n t) -> p n t", t=SLOTS), in_=adj_sb[block][:].rearrange("p t n -> p n t")
            )

        def quantize_adj(block):
            nc.vector.quantize_mx(out=adj_codes[block][:].bitcast(E4M3), scales=adj_scales[block][:], in_=adj_grouped[block][:])

        def predict_pass(bank, j, n, g):
            words = phi_sb[:, cols_of(n, 2 * N)] if g == 0 else gamma_sb[:, g - 1, cols_of(n, 2 * N)]
            plane = phi_plane[:, cols_of(n)] if g == 0 else gamma_plane[:, g - 1, cols_of(n)]
            nc.tensor.matmul_mx(
                out=bank[:],
                lhsT=xu_codes[j][:, cols_of(g, P)].bitcast(E4M3),
                lhsT_scale=xu_scales[j][:, cols_of(g, P)],
                rhs=words.bitcast(E2M1),
                rhs_scale=plane,
                start=(g == 0),
                stop=(g == PASSES - 1),
            )

        def subtract_reference(bank, j, n):
            if n == 0:
                residual[j] = staged("residual", [P, F], F32)
                e_sb[j] = staged("e_sb", [P, F], BF16)
            nc.vector.tensor_tensor(
                out=residual[j][:, cols_of(n)].rearrange("m (w p b) -> m w p b", w=2, b=2),
                in0=bank[:].rearrange("m (p w b) -> m w p b", w=2, b=2),
                in1=y_sb[j][:, cols_of(n)].rearrange("m (p w b) -> m w p b", w=2, b=2),
                op=ALU.subtract,
            )

        def predict(j, chunks):
            for n in chunks:
                bank = new_bank()
                for g in range(PASSES):
                    predict_pass(bank, j, n, g)
                subtract_reference(bank, j, n)

        plan = plan_back_projections()
        penalty_queue = [unit for i in range(TILES) for unit in plan[i] if unit not in HEAD_UNITS]
        gpsimd_weighs = [i for i in range(LAST) if plan[i]]
        deferred = []

        def penalty(unit, quantised=None):
            j, h = unit
            if quantised is None:
                own = kept("penalty%d_%d" % unit, [P, N], F32)
                penalties[unit] = own[:]
            else:
                penalties[unit] = quantised[:].bitcast(F32)[:, N // 2 :]
            nc.gpsimd.tensor_tensor(out=penalties[unit], in0=u_sb[j][:, cols_of(h)], in1=uwt_rows[:, cols_of(h)], op=ALU.mult)

        def start_penalties(count, quantised):
            batch = penalty_queue[:count]
            for unit in batch:
                penalty_queue.remove(unit)
            penalty(batch[0], quantised)
            deferred.extend(batch[1:])

        def penalties_beside(i):
            if i == LAST:
                return len(penalty_queue)
            handed_over = 1 if i in gpsimd_weighs else 0
            return gpsimd_ops_beside(2 * CHUNKS - handed_over + len(plan[i])) - handed_over

        def weigh(j):
            front, tail = slice(0, 2 * N), slice(2 * N, F)
            if j in gpsimd_weighs:
                nc.gpsimd.tensor_tensor(out=e_sb[j][:, tail], in0=residual[j][:, tail], in1=ywt_tail[:], op=ALU.mult)
            for unit in deferred:
                penalty(unit)
            deferred.clear()
            nc.vector.tensor_tensor(
                out=e_sb[j][:, front], in0=residual[j][:, front], in1=ywt_front_bank[:].bitcast(BF16), op=ALU.mult
            )
            if j not in gpsimd_weighs:
                nc.vector.tensor_tensor(
                    out=e_sb[j][:, tail], in0=residual[j][:, tail], in1=ywt_tail_bank[:].bitcast(BF16)[:, :N], op=ALU.mult
                )

        def back_project(units):
            for j, h in units:
                bank = new_bank()
                for g in range(PASSES):
                    nc.tensor.matmul_mx(
                        out=bank[:],
                        lhsT=e_codes[j][:, cols_of(g, P)].bitcast(E5M2),
                        lhsT_scale=e_scales[j][:, cols_of(g, P)],
                        rhs=adj_codes[PASSES * h + g][:].bitcast(E4M3),
                        rhs_scale=adj_scales[PASSES * h + g][:],
                        start=(g == 0),
                        stop=(g == PASSES - 1),
                    )
                parts = 2 if (j, h) == (LAST, HALVES - 1) else 1
                for part in range(parts):
                    cols = cols_of(part, N // parts)
                    result = penalties[(j, h)][:, cols]
                    nc.vector.tensor_tensor(out=result, in0=bank[:, cols], in1=result, op=ALU.add)
                    nc.sync.dma_start(out=out[rows(j), cols_of(h)][:, cols], in_=result)

        first_passes = xu_passes(0)
        transpose_and_group(first_passes[:1])
        transpose_and_group(first_passes[1:])
        spread_uwt()
        quantize_xu(0, split=1)
        penalty(HEAD_UNITS[0], xu_grouped[0])
        penalty(HEAD_UNITS[1])
        banks = [new_bank() for n in range(CHUNKS)]
        for n in range(CHUNKS):
            predict_pass(banks[n], 0, n, 0)

        def finish_first_tile(n):
            for g in range(1, PASSES):
                predict_pass(banks[n], 0, n, g)
            subtract_reference(banks[n], 0, n)

        finish_first_tile(0)
        transpose_and_group(xu_passes(1))
        finish_first_tile(1)
        quantize_xu(1)
        penalty(HEAD_UNITS[2], xu_grouped[1])
        penalty(HEAD_UNITS[3])
        finish_first_tile(2)
        spread_ywt()
        interleave_adj(0)
        weigh(0)

        predict(1, [0])
        transpose_and_group(xu_passes(2))
        interleave_adj(1)
        predict(1, [1])
        quantize_adj(0)
        quantize_xu(2)
        start_penalties(gpsimd_ops_beside(1 + CHUNKS), xu_grouped[2])
        predict(1, [2])

        for i in range(1, LAST):
            if i > 1:
                predict(i, range(CHUNKS))
            weigh(i)
            back_project(plan[i])
            ahead = i + 2
            if ahead < TILES:
                transpose_and_group(xu_passes(ahead) + e_passes(i - 1))
            else:
                transpose_and_group(e_passes(i - 1) + e_passes(i))
            if i < ADJ_BLOCKS:
                quantize_adj(i)
            if i >= E_LAG:
                quantize_e(i - E_LAG)
            if ahead < TILES:
                quantize_xu(ahead)
                start_penalties(penalties_beside(i + 1), xu_grouped[ahead])
            else:
                quantize_e(i - 1)
                start_penalties(penalties_beside(i + 1), e_grouped[i - 1])
            if i == 1:
                nc.scalar.copy(out=ywt_tail[:].bitcast(F32), in_=ywt_tail_bank[:, :PAIRS])
            if i + 1 < ADJ_BLOCKS:
                interleave_adj(i + 1)

        predict(LAST, range(CHUNKS))
        weigh(LAST)
        quantize_e(LAST - 1)
        back_project(plan[LAST][:UNITS_BEFORE_LAST_TRANSPOSES])
        transpose_and_group(e_passes(LAST))
        back_project(plan[LAST][UNITS_BEFORE_LAST_TRANSPOSES : UNITS_BEFORE_LAST_TRANSPOSES + 1])
        quantize_e(LAST)
        back_project(plan[LAST][UNITS_BEFORE_LAST_TRANSPOSES + 1 :])
